import numpy as np
import ml_dtypes


def mxq(x, axis, fmt="e4m3"):
    dtype, down = {"e4m3": (ml_dtypes.float8_e4m3fn, 7), "e5m2": (ml_dtypes.float8_e5m2, 14)}[fmt]
    v = np.moveaxis(np.asarray(x, np.float32).astype(ml_dtypes.bfloat16).astype(np.float64), axis, -1)
    blocks = v.reshape(v.shape[:-1] + (-1, 32))
    amax = np.abs(blocks).max(-1, keepdims=True)
    byte = np.maximum(np.where(amax > 0, np.frexp(amax)[1] - 1 + 127, 0) - down, 1)
    scale = np.exp2(byte - 127.0)
    codes = (blocks / scale).astype(np.float32).astype(dtype).astype(np.float64)
    return np.moveaxis((codes * scale).reshape(v.shape), -1, axis)


WIDE = False


def mx_kscale(k):
    if not WIDE:
        return np.ones(k)
    levels = np.array([10, -10, 5, -5, 0])
    if k % 512:
        return np.exp2(np.random.permutation(np.resize(levels, k // 32))).repeat(32)
    a = np.empty((k // 512, 16))
    for p in range(k // 512):
        a[p, :8] = np.random.permutation(np.resize(levels, 8))
        for g in range(8):
            far = levels[np.abs(levels - a[p, g]) >= 10]
            a[p, g + 8] = far[np.random.randint(len(far))]
    return np.exp2(a.ravel()).repeat(32)


def f64(x):
    return np.asarray(x).astype(np.float64)


def striped(idx):
    return np.tile(idx.reshape(-1, 16).T, (8, 1)).astype(np.uint16)


def unstriped(offs):
    return offs[:16].T.reshape(-1).astype(np.int64)


def pack_weight(w):
    k, n = w.shape
    w = f64(np.asarray(w, np.float32).astype(ml_dtypes.bfloat16)).reshape(k // 32, 32, n)
    amax = np.abs(w).max(1)
    byte = np.clip(np.where(amax > 0, np.frexp(amax)[1] - 1 + 127 - 7, 1), 1, 254)
    scaled = (w * np.exp2(127.0 - byte)[:, None, :]).reshape(k, n).astype(np.float32)
    words = np.ascontiguousarray(scaled.reshape(k // 512, 128, 4, n).transpose(0, 1, 3, 2)).astype(ml_dtypes.float8_e4m3fn).view(np.uint8)
    return words, np.ascontiguousarray(byte.astype(np.uint8).reshape(k // 512, 16, n))


def unpack_weight(words, scales):
    g, p, n, _ = words.shape
    vals = np.ascontiguousarray(words).view(ml_dtypes.float8_e4m3fn).astype(np.float64) * np.repeat(np.exp2(scales.astype(np.float64) - 127.0), 8, axis=1)[..., None]
    return vals.transpose(0, 1, 3, 2).reshape(g * 512, n)


def silu(v):
    return v / (1.0 + np.exp(-np.maximum(v, -700.0)))


K, T, N = 1024, 1024, 256


def setup_inputs():
    n = np.random.standard_normal
    s = mx_kscale(K)[:, None]
    packed_xT = pack_weight(n((K, T)) * s)
    return {
        "x_words": packed_xT[0],
        "x_scales": packed_xT[1],
        "w1": (n((K, N)) / np.sqrt(K) / s).astype(np.float32),
        "w2": (n((K, N)) / np.sqrt(K) / s).astype(np.float32),
        "w3": (n((K, N)) / np.sqrt(K) / s).astype(np.float32),
        "pos1": striped(np.random.permutation(T)),
        "pos2": striped(np.random.permutation(T)),
        "pos3": striped(np.random.permutation(T)),
    }


def reference(x_words, x_scales, w1, w2, w3, pos1, pos2, pos3):
    xq = unpack_weight(x_words, x_scales)
    h = mxq(f64(w3), 0, "e4m3").T @ xq
    g = mxq(f64(w1), 0, "e4m3").T @ xq
    s = mxq(f64(w2), 0, "e4m3").T @ xq
    return silu(h[:, unstriped(pos1)] * g + s) + silu(h[:, unstriped(pos2)] * g + s) + silu(h[:, unstriped(pos3)] * g + s)

@@ -1,0 +1,228 @@
+from contextlib import ExitStack
+
+import concourse.mybir as mybir
+from concourse.masks import make_identity
+
+K, T, M = 1024, 1024, 256
+FLOPS = 3 * 2 * K * T * M
+
+F32 = mybir.dt.float32
+BF16 = mybir.dt.bfloat16
+I32 = mybir.dt.int32
+U32 = mybir.dt.uint32
+U16 = mybir.dt.uint16
+U8 = mybir.dt.uint8
+FP8X4 = mybir.dt.float8_e4m3fn_x4
+SILU = mybir.ActivationFunctionType.Silu
+MULT = mybir.AluOpType.mult
+
+P = 128
+PACK = 4
+PASSES = K // (P * PACK)
+HALF = 512
+HALVES = T // HALF
+BLOCKS = M // P
+CHUNKS = [[(0, 512), (512, 512)], [(0, 512), (512, 256), (768, 256)]]
+
+
+def tile_picked_wfilmg_silu_l_kernel(
+    tc, x_words, x_scales, w1, w2, w3, pos1, pos2, pos3, out
+):
+    nc = tc.nc
+    weights = {"h": w3, "g": w1, "s": w2}
+
+    with ExitStack() as ctx:
+        keep = ctx.enter_context(tc.tile_pool(name="keep", bufs=1))
+        ring = ctx.enter_context(tc.tile_pool(name="ring", bufs=4))
+        psum = ctx.enter_context(tc.psum_pool(name="psum", bufs=1))
+
+        x_planes = keep.tile([P, T], U8, name="x_planes", align_bytes=64)
+        nc.vector.memset(x_planes[:].bitcast(I32), 0)
+        for q in range(4):
+            nc.scalar.dma_start(
+                out=x_planes[32 * q : 32 * q + 4 * PASSES, :].bitcast(I32),
+                in_=x_scales[:, 4 * q : 4 * q + 4, :].bitcast(I32),
+            )
+        warm = keep.tile([P, 8], F32, name="warm")
+        warm_out = keep.tile([P, 8], F32, name="warm_out")
+        nc.vector.memset(warm[:], 0.0)
+        nc.scalar.activation(warm_out[:], warm[:], SILU)
+
+        identity = keep.tile([P, P], F32, name="identity")
+        make_identity(nc, identity[:])
+
+        raw = {}
+        x_codes = {}
+
+        def load_w(name, b, z):
+            t = keep.tile([P, PACK, P], F32, name="raw_%s%d%d" % (name, b, z))
+            rows = weights[name][512 * z : 512 * (z + 1), P * b : P * (b + 1)]
+            nc.sync.dma_start(out=t[:], in_=rows.rearrange("(p j) n -> p j n", j=PACK))
+            raw[name, b, z] = t
+
+        def load_x(z, c):
+            t = keep.tile([P, HALF], U32, name="x_codes%d%d" % (z, c), align_bytes=64)
+            src = x_words[z].rearrange("p n t -> p (n t)")[:, PACK * HALF * c : PACK * HALF * (c + 1)]
+            nc.sync.dma_start(out=t[:].bitcast(I32), in_=src.bitcast(I32))
+            x_codes[z, c] = t
+
+        load_w("h", 0, 0)
+        load_x(0, 0)
+        load_x(0, 1)
+        load_w("g", 0, 0)
+        load_w("h", 0, 1)
+        load_x(1, 0)
+        load_w("g", 0, 1)
+        load_x(1, 1)
+        lists = []
+
+        def load_list(pos):
+            t = keep.tile([P, T // 16], U16, name="list%d" % len(lists))
+            nc.sync.dma_start(t[:], pos)
+            lists.append(t)
+
+        load_list(pos1)
+        load_w("s", 0, 0)
+        load_w("s", 0, 1)
+        load_list(pos2)
+        load_list(pos3)
+        for name, b in (("h", 1), ("g", 1), ("s", 1)):
+            for z in range(PASSES):
+                load_w(name, b, z)
+
+        grouped = {}
+        w_codes = {}
+        w_planes = {}
+
+        def cast(name, b, z, on_vector):
+            t = keep.tile([P, P * PACK], BF16, name="grouped_%s%d%d" % (name, b, z), align_bytes=64)
+            dst = t[:].rearrange("p (c i j) -> p c j i", i=4, j=PACK)
+            src = raw[name, b, z][:].rearrange("p j (c i) -> p c j i", i=4)
+            if on_vector:
+                nc.vector.tensor_copy(out=dst, in_=src)
+            else:
+                nc.scalar.copy(out=dst, in_=src)
+            grouped[name, b, z] = t
+
+        def quantize(name, b, z):
+            codes = keep.tile([P, P], U32, name="codes_%s%d%d" % (name, b, z), align_bytes=64)
+            plane = keep.tile([P, P], U8, name="plane_%s%d%d" % (name, b, z), align_bytes=64)
+            nc.vector.quantize_mx(out=codes[:].bitcast(FP8X4), scales=plane[:], in_=grouped[name, b, z][:])
+            w_codes[name, b, z] = codes
+            w_planes[name, b, z] = plane
+
+        banks = {}
+        rows = {}
+
+        def mx_pass(name, b, c, z):
+            if z == 0:
+                banks[name, b, c] = psum.tile([P, HALF], F32, name="mm", bufs=3)
+            nc.tensor.matmul_mx(
+                out=banks[name, b, c][:],
+                lhsT=w_codes[name, b, z][:].bitcast(FP8X4),
+                lhsT_scale=w_planes[name, b, z][:],
+                rhs=x_codes[z, c][:].bitcast(FP8X4),
+                rhs_scale=x_planes[4 * z : P, HALF * c : HALF * (c + 1)],
+                start=(z == 0),
+                stop=(z == PASSES - 1),
+            )
+
+        def evacuate(name, b, c, on_vector=False):
+            if (name, b) not in rows:
+                rows[name, b] = keep.tile([P, T], F32, name="rows_%s%d" % (name, b))
+            dst = rows[name, b][:, HALF * c : HALF * (c + 1)]
+            if on_vector:
+                nc.vector.tensor_copy(out=dst, in_=banks[name, b, c][:])
+            else:
+                nc.scalar.copy(out=dst, in_=banks[name, b, c][:])
+
+        def product(name, b, c):
+            for z in range(PASSES):
+                mx_pass(name, b, c, z)
+            evacuate(name, b, c)
+
+        def prepare(name, b, on_vector):
+            for z in range(PASSES):
+                cast(name, b, z, on_vector)
+            for z in range(PASSES):
+                quantize(name, b, z)
+
+        def chunk(b, start, width):
+            pieces = width // P
+            total = psum.tile([P, HALF], F32, name="total", bufs=2)
+            for d in range(3):
+                scaled = ring.tile([P, HALF], F32, name="scaled")
+                offsets = lists[d][:, start // 16 : (start + width) // 16]
+                nc.vector.tensor_tensor(
+                    scaled[:, :width], rows["h", b][:].indirect(offsets), rows["g", b][:, start : start + width], MULT
+                )
+                turned = psum.tile([P, HALF], F32, name="turned", bufs=3)
+                for j in range(pieces):
+                    nc.tensor.matmul(
+                        turned[:, P * j : P * (j + 1)],
+                        rows["s", b][:, start + P * j : start + P * (j + 1)],
+                        identity[:],
+                        start=(j == 0),
+                        stop=False,
+                        is_transpose=True,
+                    )
+                for j in range(pieces):
+                    nc.tensor.matmul(
+                        turned[:, P * j : P * (j + 1)],
+                        scaled[:, P * j : P * (j + 1)],
+                        identity[:],
+                        start=False,
+                        stop=(j == pieces - 1),
+                        is_transpose=True,
+                    )
+                active = ring.tile([P, HALF], F32, name="active")
+                nc.scalar.activation(active[:, :width], turned[:, :width], SILU)
+                for j in range(pieces):
+                    nc.tensor.matmul(
+                        total[:, P * j : P * (j + 1)],
+                        active[:, P * j : P * (j + 1)],
+                        identity[:],
+                        start=(d == 0 and j == 0),
+                        stop=(d == 2 and j == pieces - 1),
+                        is_transpose=True,
+                    )
+            result = ring.tile([P, HALF], F32, name="result")
+            nc.scalar.copy(out=result[:, :width], in_=total[:, :width])
+            nc.sync.dma_start(out=out[P * b : P * (b + 1), start : start + width], in_=result[:, :width])
+
+        cast("h", 0, 0, True)
+        quantize("h", 0, 0)
+        mx_pass("h", 0, 0, 0)
+        mx_pass("h", 0, 1, 0)
+        cast("g", 0, 0, True)
+        quantize("g", 0, 0)
+        mx_pass("g", 0, 0, 0)
+        cast("h", 0, 1, True)
+        quantize("h", 0, 1)
+        mx_pass("h", 0, 0, 1)
+        evacuate("h", 0, 0)
+        cast("g", 0, 1, True)
+        quantize("g", 0, 1)
+        mx_pass("g", 0, 0, 1)
+        evacuate("g", 0, 0, True)
+        mx_pass("h", 0, 1, 1)
+        evacuate("h", 0, 1)
+
+        prepare("s", 0, True)
+        product("s", 0, 0)
+        product("g", 0, 1)
+        prepare("h", 1, False)
+        chunk(0, *CHUNKS[0][0])
+        product("s", 0, 1)
+        prepare("g", 1, True)
+        product("h", 1, 0)
+        product("h", 1, 1)
+        prepare("s", 1, False)
+        chunk(0, *CHUNKS[0][1])
+        product("g", 1, 0)
+        product("s", 1, 0)
+        chunk(1, *CHUNKS[1][0])
+        product("g", 1, 1)
+        product("s", 1, 1)
+        chunk(1, *CHUNKS[1][1])
+        chunk(1, *CHUNKS[1][2])

@@ -15,6 +15,7 @@ U8 = mybir.dt.uint8
 FP8X4 = mybir.dt.float8_e4m3fn_x4
 SILU = mybir.ActivationFunctionType.Silu
 MULT = mybir.AluOpType.mult
+ADD = mybir.AluOpType.add
 
 P = 128
 PACK = 4
@@ -22,7 +23,9 @@ PASSES = K // (P * PACK)
 HALF = 512
 HALVES = T // HALF
 BLOCKS = M // P
-CHUNKS = [[(0, 512), (512, 512)], [(0, 512), (512, 256), (768, 256)]]
+RAW_GATES = {("s", 1, 1): (0, 3)}
+GATES = {"h":[6,1],"g":[7,1],"s":[8,1]}
+BANKS = {"h00":0,"g00":1,"s00":2,"h01":3,"g01":4,"s01":5,"u0":6,"u1":7,"u2":0,"h10":1,"h11":2,"g10":3,"g11":4,"o0":5,"u3":6,"u4":7,"s10":1,"s11":2,"u5":0,"u6":3,"u7":4,"o1":1,"u8":2,"u9":6,"o2":5,"u10":7,"o3":0}
 
 
 def tile_picked_wfilmg_silu_l_kernel(
@@ -34,12 +37,13 @@ def tile_picked_wfilmg_silu_l_kernel(
     with ExitStack() as ctx:
         keep = ctx.enter_context(tc.tile_pool(name="keep", bufs=1))
         ring = ctx.enter_context(tc.tile_pool(name="ring", bufs=4))
+        placed = ctx.enter_context(tc.tile_pool(name="placed", bufs=1))
         psum = ctx.enter_context(tc.psum_pool(name="psum", bufs=1))
 
         x_planes = keep.tile([P, T], U8, name="x_planes", align_bytes=64)
-        nc.vector.memset(x_planes[:].bitcast(I32), 0)
+        nc.gpsimd.memset(x_planes[:].bitcast(I32), 0)
         for q in range(4):
-            nc.scalar.dma_start(
+            nc.sync.dma_start(
                 out=x_planes[32 * q : 32 * q + 4 * PASSES, :].bitcast(I32),
                 in_=x_scales[:, 4 * q : 4 * q + 4, :].bitcast(I32),
             )
@@ -55,9 +59,14 @@ def tile_picked_wfilmg_silu_l_kernel(
         x_codes = {}
 
         def load_w(name, b, z):
-            t = keep.tile([P, PACK, P], F32, name="raw_%s%d%d" % (name, b, z))
+            if (name, b, z) in RAW_GATES:
+                first, count = RAW_GATES[name, b, z]
+                wide = placed.tile([P, HALF * count], F32, name="raw_%s%d%d" % (name, b, z), align_bytes=64, offset=2048 * first)
+            else:
+                wide = keep.tile([P, HALF], F32, name="raw_%s%d%d" % (name, b, z))
+            t = wide[:, :HALF].rearrange("p (j n) -> p j n", j=PACK)
             rows = weights[name][512 * z : 512 * (z + 1), P * b : P * (b + 1)]
-            nc.sync.dma_start(out=t[:], in_=rows.rearrange("(p j) n -> p j n", j=PACK))
+            nc.sync.dma_start(out=t, in_=rows.rearrange("(p j) n -> p j n", j=PACK))
             raw[name, b, z] = t
 
         def load_x(z, c):
@@ -66,14 +75,6 @@ def tile_picked_wfilmg_silu_l_kernel(
             nc.sync.dma_start(out=t[:].bitcast(I32), in_=src.bitcast(I32))
             x_codes[z, c] = t
 
-        load_w("h", 0, 0)
-        load_x(0, 0)
-        load_x(0, 1)
-        load_w("g", 0, 0)
-        load_w("h", 0, 1)
-        load_x(1, 0)
-        load_w("g", 0, 1)
-        load_x(1, 1)
         lists = []
 
         def load_list(pos):
@@ -81,23 +82,35 @@ def tile_picked_wfilmg_silu_l_kernel(
             nc.sync.dma_start(t[:], pos)
             lists.append(t)
 
-        load_list(pos1)
+        load_w("h", 0, 0)
+        load_x(0, 0)
+        load_w("g", 0, 0)
+        load_w("h", 0, 1)
+        load_w("g", 0, 1)
+        load_x(1, 0)
         load_w("s", 0, 0)
         load_w("s", 0, 1)
+        load_x(0, 1)
+        load_x(1, 1)
+        load_list(pos1)
         load_list(pos2)
         load_list(pos3)
-        for name, b in (("h", 1), ("g", 1), ("s", 1)):
-            for z in range(PASSES):
-                load_w(name, b, z)
+        load_w("h", 1, 0)
+        load_w("h", 1, 1)
+        load_w("g", 1, 0)
+        load_w("g", 1, 1)
+        load_w("s", 1, 0)
+        load_w("s", 1, 1)
 
         grouped = {}
         w_codes = {}
         w_planes = {}
 
         def cast(name, b, z, on_vector):
-            t = keep.tile([P, P * PACK], BF16, name="grouped_%s%d%d" % (name, b, z), align_bytes=64)
+            tag = "grouped_%s%d%d" % (name, b, z)
+            t = keep.tile([P, P * PACK], BF16, name=tag, align_bytes=64)
             dst = t[:].rearrange("p (c i j) -> p c j i", i=4, j=PACK)
-            src = raw[name, b, z][:].rearrange("p j (c i) -> p c j i", i=4)
+            src = raw[name, b, z].rearrange("p j (c i) -> p c j i", i=4)
             if on_vector:
                 nc.vector.tensor_copy(out=dst, in_=src)
             else:
@@ -105,22 +118,42 @@ def tile_picked_wfilmg_silu_l_kernel(
             grouped[name, b, z] = t
 
         def quantize(name, b, z):
-            codes = keep.tile([P, P], U32, name="codes_%s%d%d" % (name, b, z), align_bytes=64)
+            tag = "codes_%s%d%d" % (name, b, z)
+            codes = keep.tile([P, P], U32, name=tag, align_bytes=64)
             plane = keep.tile([P, P], U8, name="plane_%s%d%d" % (name, b, z), align_bytes=64)
             nc.vector.quantize_mx(out=codes[:].bitcast(FP8X4), scales=plane[:], in_=grouped[name, b, z][:])
-            w_codes[name, b, z] = codes
-            w_planes[name, b, z] = plane
+            w_codes[name, b, z] = codes[:]
+            w_planes[name, b, z] = plane[:]
+
+        def cast_wide(name, z, on_vector):
+            if z == 0:
+                first, count = GATES[name]
+                grouped[name] = placed.tile([P, 1024 * count], BF16, name="grouped_%s1" % name, align_bytes=64, offset=2048 * first)
+            dst = grouped[name][:, P * PACK * z : P * PACK * (z + 1)].rearrange("p (c i j) -> p c j i", i=4, j=PACK)
+            src = raw[name, 1, z].rearrange("p j (c i) -> p c j i", i=4)
+            if on_vector:
+                nc.vector.tensor_copy(out=dst, in_=src)
+            else:
+                nc.scalar.copy(out=dst, in_=src)
+
+        def quantize_wide(name):
+            codes = keep.tile([P, PASSES * P], U32, name="codes_%s1" % name, align_bytes=64)
+            plane = keep.tile([P, PASSES * P], U8, name="plane_%s1" % name, align_bytes=64)
+            nc.vector.quantize_mx(out=codes[:].bitcast(FP8X4), scales=plane[:], in_=grouped[name][:, :1024])
+            for z in range(PASSES):
+                w_codes[name, 1, z] = codes[:, P * z : P * (z + 1)]
+                w_planes[name, 1, z] = plane[:, P * z : P * (z + 1)]
 
         banks = {}
         rows = {}
 
         def mx_pass(name, b, c, z):
             if z == 0:
-                banks[name, b, c] = psum.tile([P, HALF], F32, name="mm", bufs=3)
+                banks[name, b, c] = psum.tile([P, HALF], F32, name="mx_%s%d%d" % (name, b, c), offset=2048 * BANKS[name + str(b) + str(c)])
             nc.tensor.matmul_mx(
                 out=banks[name, b, c][:],
-                lhsT=w_codes[name, b, z][:].bitcast(FP8X4),
-                lhsT_scale=w_planes[name, b, z][:],
+                lhsT=w_codes[name, b, z].bitcast(FP8X4),
+                lhsT_scale=w_planes[name, b, z],
                 rhs=x_codes[z, c][:].bitcast(FP8X4),
                 rhs_scale=x_planes[4 * z : P, HALF * c : HALF * (c + 1)],
                 start=(z == 0),
@@ -147,82 +180,196 @@ def tile_picked_wfilmg_silu_l_kernel(
             for z in range(PASSES):
                 quantize(name, b, z)
 
-        def chunk(b, start, width):
-            pieces = width // P
-            total = psum.tile([P, HALF], F32, name="total", bufs=2)
-            for d in range(3):
-                scaled = ring.tile([P, HALF], F32, name="scaled")
-                offsets = lists[d][:, start // 16 : (start + width) // 16]
-                nc.vector.tensor_tensor(
-                    scaled[:, :width], rows["h", b][:].indirect(offsets), rows["g", b][:, start : start + width], MULT
+        units = [
+            (0, 0, 512, 0, True), (0, 0, 512, 1, True), (0, 0, 512, 2, True),
+            (0, 512, 512, 0, True), (0, 512, 512, 1, True), (0, 512, 512, 2, True),
+            (1, 0, 512, 0, True), (1, 0, 512, 1, True), (1, 0, 512, 2, True),
+            (1, 512, 512, 0, True), (1, 512, 512, 1, True), (1, 512, 256, 2, False), (1, 768, 256, 2, False),
+        ]
+        closes = [2, 5, 8, 10]
+        slots = [3,4,0,1,2,0,1,2,0,1,2,0,0.5]
+        scaled = {}
+        turned = {}
+        active = {}
+        totals = {}
+
+        def gather(u):
+            b, start, width, d, on_tensor = units[u]
+            scaled[u] = placed.tile([P, units[u][2]], F32, name="scaled%d" % u, align_bytes=64, offset=int(2048 * slots[u]))
+            offsets = lists[d][:, start // 16 : (start + width) // 16]
+            nc.vector.tensor_tensor(
+                scaled[u][:, :width], rows["h", b][:].indirect(offsets), rows["g", b][:, start : start + width], MULT
+            )
+
+        def turn_shift(u):
+            b, start, width, d, on_tensor = units[u]
+            turned[u] = psum.tile([P, HALF], F32, name="turned%d" % u, offset=2048 * BANKS["u" + str(u)])
+            for j in range(width // P):
+                nc.tensor.matmul(
+                    turned[u][:, P * j : P * (j + 1)],
+                    rows["s", b][:, start + P * j : start + P * (j + 1)],
+                    identity[:],
+                    start=(j == 0),
+                    stop=False,
+                    is_transpose=True,
                 )
-                turned = psum.tile([P, HALF], F32, name="turned", bufs=3)
-                for j in range(pieces):
-                    nc.tensor.matmul(
-                        turned[:, P * j : P * (j + 1)],
-                        rows["s", b][:, start + P * j : start + P * (j + 1)],
-                        identity[:],
-                        start=(j == 0),
-                        stop=False,
-                        is_transpose=True,
-                    )
-                for j in range(pieces):
-                    nc.tensor.matmul(
-                        turned[:, P * j : P * (j + 1)],
-                        scaled[:, P * j : P * (j + 1)],
-                        identity[:],
-                        start=False,
-                        stop=(j == pieces - 1),
-                        is_transpose=True,
-                    )
-                active = ring.tile([P, HALF], F32, name="active")
-                nc.scalar.activation(active[:, :width], turned[:, :width], SILU)
-                for j in range(pieces):
-                    nc.tensor.matmul(
-                        total[:, P * j : P * (j + 1)],
-                        active[:, P * j : P * (j + 1)],
-                        identity[:],
-                        start=(d == 0 and j == 0),
-                        stop=(d == 2 and j == pieces - 1),
-                        is_transpose=True,
-                    )
+
+        def turn_scaled(u):
+            b, start, width, d, on_tensor = units[u]
+            for j in range(width // P):
+                nc.tensor.matmul(
+                    turned[u][:, P * j : P * (j + 1)],
+                    scaled[u][:, P * j : P * (j + 1)],
+                    identity[:],
+                    start=False,
+                    stop=(j == width // P - 1),
+                    is_transpose=True,
+                )
+            active[u] = ring.tile([P, HALF], F32, name="active", bufs=4)
+            nc.scalar.activation(active[u][:, :width], turned[u][:, :width], SILU)
+
+        def turn_back(u):
+            b, start, width, d, on_tensor = units[u]
+            if d == 0:
+                totals[b, start] = psum.tile([P, HALF], F32, name="total%d" % u, offset=2048 * BANKS["o" + str(u // 3)])
+            total = totals[b, start]
+            for j in range(width // P):
+                nc.tensor.matmul(
+                    total[:, P * j : P * (j + 1)],
+                    active[u][:, P * j : P * (j + 1)],
+                    identity[:],
+                    start=(d == 0 and j == 0),
+                    stop=(u in closes and j == width // P - 1),
+                    is_transpose=True,
+                )
+
+        def store(u):
+            b, start, width, d, on_tensor = units[u]
             result = ring.tile([P, HALF], F32, name="result")
-            nc.scalar.copy(out=result[:, :width], in_=total[:, :width])
+            nc.scalar.copy(out=result[:, :width], in_=totals[b, start][:, :width])
+            nc.sync.dma_start(out=out[P * b : P * (b + 1), start : start + width], in_=result[:, :width])
+
+        def shift_on_vector(u):
+            b, start, width, d, on_tensor = units[u]
+            shifted = ring.tile([P, HALF], F32, name="shifted", bufs=2)
+            nc.vector.tensor_tensor(shifted[:, :width], scaled[u][:, :width], rows["s", b][:, start : start + width], ADD)
+            active[u] = ring.tile([P, HALF], F32, name="active", bufs=4)
+            nc.scalar.activation(active[u][:, :width], shifted[:, :width], SILU)
+
+        def finish_on_vector(u):
+            b, start, width, d, on_tensor = units[u]
+            first = start - start % HALF
+            result = ring.tile([P, HALF], F32, name="result")
+            nc.vector.tensor_tensor(
+                result[:, :width], totals[b, first][:, start - first : start - first + width], active[u][:, :width], ADD
+            )
             nc.sync.dma_start(out=out[P * b : P * (b + 1), start : start + width], in_=result[:, :width])
 
         cast("h", 0, 0, True)
         quantize("h", 0, 0)
         mx_pass("h", 0, 0, 0)
-        mx_pass("h", 0, 1, 0)
         cast("g", 0, 0, True)
         quantize("g", 0, 0)
         mx_pass("g", 0, 0, 0)
         cast("h", 0, 1, True)
         quantize("h", 0, 1)
-        mx_pass("h", 0, 0, 1)
-        evacuate("h", 0, 0)
         cast("g", 0, 1, True)
         quantize("g", 0, 1)
+        mx_pass("h", 0, 0, 1)
+        evacuate("h", 0, 0)
         mx_pass("g", 0, 0, 1)
-        evacuate("g", 0, 0, True)
+        evacuate("g", 0, 0)
+        cast("s", 0, 0, True)
+        quantize("s", 0, 0)
+        cast("s", 0, 1, True)
+        quantize("s", 0, 1)
+        mx_pass("s", 0, 0, 0)
+        mx_pass("h", 0, 1, 0)
         mx_pass("h", 0, 1, 1)
-        evacuate("h", 0, 1)
-
-        prepare("s", 0, True)
-        product("s", 0, 0)
+        evacuate("h", 0, 1, True)
+        mx_pass("s", 0, 0, 1)
+        evacuate("s", 0, 0)
         product("g", 0, 1)
-        prepare("h", 1, False)
-        chunk(0, *CHUNKS[0][0])
-        product("s", 0, 1)
-        prepare("g", 1, True)
-        product("h", 1, 0)
-        product("h", 1, 1)
-        prepare("s", 1, False)
-        chunk(0, *CHUNKS[0][1])
-        product("g", 1, 0)
-        product("s", 1, 0)
-        chunk(1, *CHUNKS[1][0])
-        product("g", 1, 1)
-        product("s", 1, 1)
-        chunk(1, *CHUNKS[1][1])
-        chunk(1, *CHUNKS[1][2])
+        mx_pass("s", 0, 1, 0)
+        mx_pass("s", 0, 1, 1)
+        gather(0)
+        turn_shift(0)
+        turn_shift(1)
+        turn_shift(2)
+        cast_wide("h", 0, False)
+        cast_wide("h", 1, False)
+        evacuate("s", 0, 1)
+        gather(1)
+        turn_scaled(0)
+        quantize_wide("h")
+        cast_wide("g", 0, True)
+        cast_wide("g", 1, True)
+        cast_wide("s", 0, True)
+        cast_wide("s", 1, True)
+        quantize_wide("g")
+        quantize_wide("s")
+        turn_scaled(1)
+        mx_pass("h", 1, 0, 0)
+        mx_pass("h", 1, 0, 1)
+        mx_pass("h", 1, 1, 0)
+        mx_pass("h", 1, 1, 1)
+        evacuate("h", 1, 0)
+        evacuate("h", 1, 1)
+        turn_back(0)
+        turn_shift(3)
+        gather(2)
+        mx_pass("g", 1, 0, 0)
+        mx_pass("g", 1, 0, 1)
+        mx_pass("g", 1, 1, 0)
+        mx_pass("g", 1, 1, 1)
+        evacuate("g", 1, 0)
+        mx_pass("s", 1, 0, 0)
+        mx_pass("s", 1, 0, 1)
+        mx_pass("s", 1, 1, 0)
+        mx_pass("s", 1, 1, 1)
+        turn_scaled(2)
+        gather(3)
+        evacuate("g", 1, 1)
+        turn_back(1)
+        turn_shift(4)
+        evacuate("s", 1, 0)
+        turn_scaled(3)
+        gather(4)
+        evacuate("s", 1, 1)
+        turn_back(2)
+        turn_shift(5)
+        turn_scaled(4)
+        gather(5)
+        store(2)
+        turn_back(3)
+        turn_shift(6)
+        turn_scaled(5)
+        gather(6)
+        turn_shift(7)
+        turn_back(4)
+        turn_shift(8)
+        turn_scaled(6)
+        gather(7)
+        turn_back(5)
+        turn_shift(9)
+        turn_scaled(7)
+        store(5)
+        gather(8)
+        turn_back(6)
+        turn_shift(10)
+        turn_scaled(8)
+        gather(9)
+        turn_back(7)
+        turn_scaled(9)
+        gather(10)
+        turn_scaled(10)
+        turn_back(8)
+        gather(11)
+        gather(12)
+        turn_back(9)
+        shift_on_vector(11)
+        store(8)
+        shift_on_vector(12)
+        turn_back(10)
+        finish_on_vector(11)
+        finish_on_vector(12)

@@ -23,9 +23,9 @@ PASSES = K // (P * PACK)
 HALF = 512
 HALVES = T // HALF
 BLOCKS = M // P
-RAW_GATES = {("s", 1, 1): (0, 3)}
-GATES = {"h":[6,1],"g":[7,1],"s":[8,1]}
-BANKS = {"h00":0,"g00":1,"s00":2,"h01":3,"g01":4,"s01":5,"u0":6,"u1":7,"u2":0,"h10":1,"h11":2,"g10":3,"g11":4,"o0":5,"u3":6,"u4":7,"s10":1,"s11":2,"u5":0,"u6":3,"u7":4,"o1":1,"u8":2,"u9":6,"o2":5,"u10":7,"o3":0}
+RAW_GATES = {("s", 1, 1): (2, 3)}
+GATES = {"h":[0,1],"g":[1,1],"s":[10,1]}
+BANKS = {"h00":3,"g00":5,"s00":2,"h01":6,"g01":5,"u0":7,"u1":4,"u2":3,"s01":6,"h10":5,"o0":2,"u3":3,"h11":7,"u4":5,"g10":4,"u5":1,"s10":0,"o1":6,"u6":4,"g11":5,"u7":2,"s11":0,"o2":5,"u9":0,"u10":1,"o3":0,"u8":3,"y8":14,"a8":3,"y11":7,"a11":14}
 
 
 def tile_picked_wfilmg_silu_l_kernel(
@@ -36,7 +36,6 @@ def tile_picked_wfilmg_silu_l_kernel(
 
     with ExitStack() as ctx:
         keep = ctx.enter_context(tc.tile_pool(name="keep", bufs=1))
-        ring = ctx.enter_context(tc.tile_pool(name="ring", bufs=4))
         placed = ctx.enter_context(tc.tile_pool(name="placed", bufs=1))
         psum = ctx.enter_context(tc.psum_pool(name="psum", bufs=1))
 
@@ -75,32 +74,13 @@ def tile_picked_wfilmg_silu_l_kernel(
             nc.sync.dma_start(out=t[:].bitcast(I32), in_=src.bitcast(I32))
             x_codes[z, c] = t
 
-        lists = []
+        lists = {}
 
-        def load_list(pos):
-            t = keep.tile([P, T // 16], U16, name="list%d" % len(lists))
+        def load_list(d, pos):
+            t = keep.tile([P, T // 16], U16, name="list%d" % d)
             nc.sync.dma_start(t[:], pos)
-            lists.append(t)
+            lists[d] = t
 
-        load_w("h", 0, 0)
-        load_x(0, 0)
-        load_w("g", 0, 0)
-        load_w("h", 0, 1)
-        load_w("g", 0, 1)
-        load_x(1, 0)
-        load_w("s", 0, 0)
-        load_w("s", 0, 1)
-        load_x(0, 1)
-        load_x(1, 1)
-        load_list(pos1)
-        load_list(pos2)
-        load_list(pos3)
-        load_w("h", 1, 0)
-        load_w("h", 1, 1)
-        load_w("g", 1, 0)
-        load_w("g", 1, 1)
-        load_w("s", 1, 0)
-        load_w("s", 1, 1)
 
         grouped = {}
         w_codes = {}
@@ -126,7 +106,7 @@ def tile_picked_wfilmg_silu_l_kernel(
             w_planes[name, b, z] = plane[:]
 
         def cast_wide(name, z, on_vector):
-            if z == 0:
+            if name not in grouped:
                 first, count = GATES[name]
                 grouped[name] = placed.tile([P, 1024 * count], BF16, name="grouped_%s1" % name, align_bytes=64, offset=2048 * first)
             dst = grouped[name][:, P * PACK * z : P * PACK * (z + 1)].rearrange("p (c i j) -> p c j i", i=4, j=PACK)
@@ -183,11 +163,11 @@ def tile_picked_wfilmg_silu_l_kernel(
         units = [
             (0, 0, 512, 0, True), (0, 0, 512, 1, True), (0, 0, 512, 2, True),
             (0, 512, 512, 0, True), (0, 512, 512, 1, True), (0, 512, 512, 2, True),
-            (1, 0, 512, 0, True), (1, 0, 512, 1, True), (1, 0, 512, 2, True),
+            (1, 0, 512, 0, True), (1, 0, 512, 1, True), (1, 0, 512, 2, False),
             (1, 512, 512, 0, True), (1, 512, 512, 1, True), (1, 512, 256, 2, False), (1, 768, 256, 2, False),
         ]
-        closes = [2, 5, 8, 10]
-        slots = [3,4,0,1,2,0,1,2,0,1,2,0,0.5]
+        closes = [2,5,7,10]
+        slots = [5,8,0,4,3,0,5,3,4,2,7,8,8.5]
         scaled = {}
         turned = {}
         active = {}
@@ -225,7 +205,7 @@ def tile_picked_wfilmg_silu_l_kernel(
                     stop=(j == width // P - 1),
                     is_transpose=True,
                 )
-            active[u] = ring.tile([P, HALF], F32, name="active", bufs=4)
+            active[u] = placed.tile([P, width], F32, name="active%d" % u, align_bytes=64, offset=2048 * (11 + u))
             nc.scalar.activation(active[u][:, :width], turned[u][:, :width], SILU)
 
         def turn_back(u):
@@ -245,131 +225,150 @@ def tile_picked_wfilmg_silu_l_kernel(
 
         def store(u):
             b, start, width, d, on_tensor = units[u]
-            result = ring.tile([P, HALF], F32, name="result")
+            result = keep.tile([P, width], F32, name="result%d" % u)
             nc.scalar.copy(out=result[:, :width], in_=totals[b, start][:, :width])
             nc.sync.dma_start(out=out[P * b : P * (b + 1), start : start + width], in_=result[:, :width])
 
         def shift_on_vector(u):
             b, start, width, d, on_tensor = units[u]
-            shifted = ring.tile([P, HALF], F32, name="shifted", bufs=2)
+            shifted = placed.tile([P, width], F32, name="shifted%d" % u, align_bytes=64, offset=2048 * BANKS["y%d" % min(u, 11)] + 1024 * (u == 12))
             nc.vector.tensor_tensor(shifted[:, :width], scaled[u][:, :width], rows["s", b][:, start : start + width], ADD)
-            active[u] = ring.tile([P, HALF], F32, name="active", bufs=4)
+            active[u] = placed.tile([P, width], F32, name="active%d" % u, align_bytes=64, offset=2048 * BANKS["a%d" % min(u, 11)] + 1024 * (u == 12))
             nc.scalar.activation(active[u][:, :width], shifted[:, :width], SILU)
 
         def finish_on_vector(u):
             b, start, width, d, on_tensor = units[u]
             first = start - start % HALF
-            result = ring.tile([P, HALF], F32, name="result")
+            result = keep.tile([P, width], F32, name="result%d" % u)
             nc.vector.tensor_tensor(
                 result[:, :width], totals[b, first][:, start - first : start - first + width], active[u][:, :width], ADD
             )
             nc.sync.dma_start(out=out[P * b : P * (b + 1), start : start + width], in_=result[:, :width])
 
-        cast("h", 0, 0, True)
-        quantize("h", 0, 0)
-        mx_pass("h", 0, 0, 0)
-        cast("g", 0, 0, True)
+        load_w("g", 0, 0)
+        load_x(0, 0)
+        load_w("h", 0, 0)
+        load_w("h", 0, 1)
+        load_w("g", 0, 1)
+        load_x(1, 0)
+        load_w("s", 0, 0)
+        load_x(0, 1)
+        load_w("s", 0, 1)
+        load_x(1, 1)
+        load_w("h", 1, 1)
+        load_list(0, pos1)
+        load_w("g", 1, 0)
+        load_w("s", 1, 0)
+        load_list(1, pos2)
+        load_w("h", 1, 0)
+        load_list(2, pos3)
+        load_w("g", 1, 1)
+        load_w("s", 1, 1)
+        cast("g", 0, 0, False)
         quantize("g", 0, 0)
         mx_pass("g", 0, 0, 0)
+        cast("h", 0, 0, True)
+        quantize("h", 0, 0)
         cast("h", 0, 1, True)
+        mx_pass("h", 0, 0, 0)
         quantize("h", 0, 1)
         cast("g", 0, 1, True)
-        quantize("g", 0, 1)
         mx_pass("h", 0, 0, 1)
-        evacuate("h", 0, 0)
+        quantize("g", 0, 1)
+        cast("s", 0, 0, False)
         mx_pass("g", 0, 0, 1)
+        evacuate("h", 0, 0, True)
+        mx_pass("h", 0, 1, 0)
         evacuate("g", 0, 0)
-        cast("s", 0, 0, True)
         quantize("s", 0, 0)
         cast("s", 0, 1, True)
-        quantize("s", 0, 1)
         mx_pass("s", 0, 0, 0)
-        mx_pass("h", 0, 1, 0)
+        quantize("s", 0, 1)
         mx_pass("h", 0, 1, 1)
+        mx_pass("g", 0, 1, 0)
+        mx_pass("g", 0, 1, 1)
+        cast_wide("h", 1, False)
         evacuate("h", 0, 1, True)
         mx_pass("s", 0, 0, 1)
-        evacuate("s", 0, 0)
-        product("g", 0, 1)
+        evacuate("g", 0, 1)
+        cast_wide("g", 0, True)
         mx_pass("s", 0, 1, 0)
         mx_pass("s", 0, 1, 1)
         gather(0)
+        evacuate("s", 0, 0)
+        cast_wide("s", 0, False)
         turn_shift(0)
-        turn_shift(1)
-        turn_shift(2)
-        cast_wide("h", 0, False)
-        cast_wide("h", 1, False)
-        evacuate("s", 0, 1)
         gather(1)
+        cast_wide("h", 0, False)
+        turn_shift(2)
         turn_scaled(0)
+        evacuate("s", 0, 1)
+        turn_shift(1)
         quantize_wide("h")
-        cast_wide("g", 0, True)
-        cast_wide("g", 1, True)
-        cast_wide("s", 0, True)
-        cast_wide("s", 1, True)
-        quantize_wide("g")
-        quantize_wide("s")
+        cast_wide("g", 1, False)
         turn_scaled(1)
+        gather(2)
         mx_pass("h", 1, 0, 0)
         mx_pass("h", 1, 0, 1)
-        mx_pass("h", 1, 1, 0)
-        mx_pass("h", 1, 1, 1)
-        evacuate("h", 1, 0)
-        evacuate("h", 1, 1)
         turn_back(0)
-        turn_shift(3)
-        gather(2)
-        mx_pass("g", 1, 0, 0)
-        mx_pass("g", 1, 0, 1)
-        mx_pass("g", 1, 1, 0)
-        mx_pass("g", 1, 1, 1)
-        evacuate("g", 1, 0)
-        mx_pass("s", 1, 0, 0)
-        mx_pass("s", 1, 0, 1)
-        mx_pass("s", 1, 1, 0)
-        mx_pass("s", 1, 1, 1)
+        cast_wide("s", 1, True)
+        evacuate("h", 1, 0)
+        quantize_wide("g")
         turn_scaled(2)
         gather(3)
-        evacuate("g", 1, 1)
+        mx_pass("h", 1, 1, 0)
+        mx_pass("h", 1, 1, 1)
+        quantize_wide("s")
         turn_back(1)
-        turn_shift(4)
-        evacuate("s", 1, 0)
-        turn_scaled(3)
+        evacuate("h", 1, 1)
+        turn_shift(3)
         gather(4)
-        evacuate("s", 1, 1)
+        mx_pass("g", 1, 0, 0)
+        mx_pass("g", 1, 0, 1)
+        turn_scaled(3)
+        gather(5)
+        evacuate("g", 1, 0)
+        turn_shift(4)
         turn_back(2)
         turn_shift(5)
-        turn_scaled(4)
-        gather(5)
-        store(2)
-        turn_back(3)
-        turn_shift(6)
-        turn_scaled(5)
         gather(6)
-        turn_shift(7)
+        store(2)
+        turn_scaled(4)
+        mx_pass("s", 1, 0, 0)
+        mx_pass("s", 1, 0, 1)
+        gather(8)
+        turn_scaled(5)
+        evacuate("s", 1, 0)
+        turn_back(3)
         turn_back(4)
-        turn_shift(8)
-        turn_scaled(6)
+        mx_pass("g", 1, 1, 0)
+        mx_pass("g", 1, 1, 1)
         gather(7)
         turn_back(5)
-        turn_shift(9)
-        turn_scaled(7)
+        evacuate("g", 1, 1)
+        turn_shift(6)
+        shift_on_vector(8)
+        turn_scaled(6)
         store(5)
-        gather(8)
-        turn_back(6)
-        turn_shift(10)
-        turn_scaled(8)
+        mx_pass("s", 1, 1, 0)
+        mx_pass("s", 1, 1, 1)
         gather(9)
-        turn_back(7)
-        turn_scaled(9)
+        turn_shift(7)
+        evacuate("s", 1, 1)
+        turn_back(6)
         gather(10)
-        turn_scaled(10)
-        turn_back(8)
-        gather(11)
+        turn_scaled(7)
+        turn_shift(10)
+        turn_shift(9)
+        turn_scaled(9)
         gather(12)
+        turn_scaled(10)
+        turn_back(7)
+        gather(11)
+        shift_on_vector(12)
         turn_back(9)
         shift_on_vector(11)
-        store(8)
-        shift_on_vector(12)
+        finish_on_vector(8)
         turn_back(10)
-        finish_on_vector(11)
         finish_on_vector(12)
+        finish_on_vector(11)

from contextlib import ExitStack

import concourse.mybir as mybir
from concourse.masks import make_identity

K, T, M = 1024, 1024, 256
FLOPS = 3 * 2 * K * T * M

F32 = mybir.dt.float32
BF16 = mybir.dt.bfloat16
I32 = mybir.dt.int32
U32 = mybir.dt.uint32
U16 = mybir.dt.uint16
U8 = mybir.dt.uint8
FP8X4 = mybir.dt.float8_e4m3fn_x4
SILU = mybir.ActivationFunctionType.Silu
MULT = mybir.AluOpType.mult
ADD = mybir.AluOpType.add

P = 128
PACK = 4
PASSES = K // (P * PACK)
HALF = 512
HALVES = T // HALF
BLOCKS = M // P
RAW_GATES = {("s", 1, 1): (2, 3)}
GATES = {"h":[0,1],"g":[1,1],"s":[10,1]}
BANKS = {"h00":3,"g00":5,"s00":2,"h01":6,"g01":5,"u0":7,"u1":4,"u2":3,"s01":6,"h10":5,"o0":2,"u3":3,"h11":7,"u4":5,"g10":4,"u5":1,"s10":0,"o1":6,"u6":4,"g11":5,"u7":2,"s11":0,"o2":5,"u9":0,"u10":1,"o3":0,"u8":3,"y8":14,"a8":3,"y11":7,"a11":14}


def tile_picked_wfilmg_silu_l_kernel(
    tc, x_words, x_scales, w1, w2, w3, pos1, pos2, pos3, out
):
    nc = tc.nc
    weights = {"h": w3, "g": w1, "s": w2}

    with ExitStack() as ctx:
        keep = ctx.enter_context(tc.tile_pool(name="keep", bufs=1))
        placed = ctx.enter_context(tc.tile_pool(name="placed", bufs=1))
        psum = ctx.enter_context(tc.psum_pool(name="psum", bufs=1))

        x_planes = keep.tile([P, T], U8, name="x_planes", align_bytes=64)
        nc.gpsimd.memset(x_planes[:].bitcast(I32), 0)
        for q in range(4):
            nc.sync.dma_start(
                out=x_planes[32 * q : 32 * q + 4 * PASSES, :].bitcast(I32),
                in_=x_scales[:, 4 * q : 4 * q + 4, :].bitcast(I32),
            )
        warm = keep.tile([P, 8], F32, name="warm")
        warm_out = keep.tile([P, 8], F32, name="warm_out")
        nc.vector.memset(warm[:], 0.0)
        nc.scalar.activation(warm_out[:], warm[:], SILU)

        identity = keep.tile([P, P], F32, name="identity")
        make_identity(nc, identity[:])

        raw = {}
        x_codes = {}

        def load_w(name, b, z):
            if (name, b, z) in RAW_GATES:
                first, count = RAW_GATES[name, b, z]
                wide = placed.tile([P, HALF * count], F32, name="raw_%s%d%d" % (name, b, z), align_bytes=64, offset=2048 * first)
            else:
                wide = keep.tile([P, HALF], F32, name="raw_%s%d%d" % (name, b, z))
            t = wide[:, :HALF].rearrange("p (j n) -> p j n", j=PACK)
            rows = weights[name][512 * z : 512 * (z + 1), P * b : P * (b + 1)]
            nc.sync.dma_start(out=t, in_=rows.rearrange("(p j) n -> p j n", j=PACK))
            raw[name, b, z] = t

        def load_x(z, c):
            t = keep.tile([P, HALF], U32, name="x_codes%d%d" % (z, c), align_bytes=64)
            src = x_words[z].rearrange("p n t -> p (n t)")[:, PACK * HALF * c : PACK * HALF * (c + 1)]
            nc.sync.dma_start(out=t[:].bitcast(I32), in_=src.bitcast(I32))
            x_codes[z, c] = t

        lists = {}

        def load_list(d, pos):
            t = keep.tile([P, T // 16], U16, name="list%d" % d)
            nc.sync.dma_start(t[:], pos)
            lists[d] = t


        grouped = {}
        w_codes = {}
        w_planes = {}

        def cast(name, b, z, on_vector):
            tag = "grouped_%s%d%d" % (name, b, z)
            t = keep.tile([P, P * PACK], BF16, name=tag, align_bytes=64)
            dst = t[:].rearrange("p (c i j) -> p c j i", i=4, j=PACK)
            src = raw[name, b, z].rearrange("p j (c i) -> p c j i", i=4)
            if on_vector:
                nc.vector.tensor_copy(out=dst, in_=src)
            else:
                nc.scalar.copy(out=dst, in_=src)
            grouped[name, b, z] = t

        def quantize(name, b, z):
            tag = "codes_%s%d%d" % (name, b, z)
            codes = keep.tile([P, P], U32, name=tag, align_bytes=64)
            plane = keep.tile([P, P], U8, name="plane_%s%d%d" % (name, b, z), align_bytes=64)
            nc.vector.quantize_mx(out=codes[:].bitcast(FP8X4), scales=plane[:], in_=grouped[name, b, z][:])
            w_codes[name, b, z] = codes[:]
            w_planes[name, b, z] = plane[:]

        def cast_wide(name, z, on_vector):
            if name not in grouped:
                first, count = GATES[name]
                grouped[name] = placed.tile([P, 1024 * count], BF16, name="grouped_%s1" % name, align_bytes=64, offset=2048 * first)
            dst = grouped[name][:, P * PACK * z : P * PACK * (z + 1)].rearrange("p (c i j) -> p c j i", i=4, j=PACK)
            src = raw[name, 1, z].rearrange("p j (c i) -> p c j i", i=4)
            if on_vector:
                nc.vector.tensor_copy(out=dst, in_=src)
            else:
                nc.scalar.copy(out=dst, in_=src)

        def quantize_wide(name):
            codes = keep.tile([P, PASSES * P], U32, name="codes_%s1" % name, align_bytes=64)
            plane = keep.tile([P, PASSES * P], U8, name="plane_%s1" % name, align_bytes=64)
            nc.vector.quantize_mx(out=codes[:].bitcast(FP8X4), scales=plane[:], in_=grouped[name][:, :1024])
            for z in range(PASSES):
                w_codes[name, 1, z] = codes[:, P * z : P * (z + 1)]
                w_planes[name, 1, z] = plane[:, P * z : P * (z + 1)]

        banks = {}
        rows = {}

        def mx_pass(name, b, c, z):
            if z == 0:
                banks[name, b, c] = psum.tile([P, HALF], F32, name="mx_%s%d%d" % (name, b, c), offset=2048 * BANKS[name + str(b) + str(c)])
            nc.tensor.matmul_mx(
                out=banks[name, b, c][:],
                lhsT=w_codes[name, b, z].bitcast(FP8X4),
                lhsT_scale=w_planes[name, b, z],
                rhs=x_codes[z, c][:].bitcast(FP8X4),
                rhs_scale=x_planes[4 * z : P, HALF * c : HALF * (c + 1)],
                start=(z == 0),
                stop=(z == PASSES - 1),
            )

        def evacuate(name, b, c, on_vector=False):
            if (name, b) not in rows:
                rows[name, b] = keep.tile([P, T], F32, name="rows_%s%d" % (name, b))
            dst = rows[name, b][:, HALF * c : HALF * (c + 1)]
            if on_vector:
                nc.vector.tensor_copy(out=dst, in_=banks[name, b, c][:])
            else:
                nc.scalar.copy(out=dst, in_=banks[name, b, c][:])

        def product(name, b, c):
            for z in range(PASSES):
                mx_pass(name, b, c, z)
            evacuate(name, b, c)

        def prepare(name, b, on_vector):
            for z in range(PASSES):
                cast(name, b, z, on_vector)
            for z in range(PASSES):
                quantize(name, b, z)

        units = [
            (0, 0, 512, 0, True), (0, 0, 512, 1, True), (0, 0, 512, 2, True),
            (0, 512, 512, 0, True), (0, 512, 512, 1, True), (0, 512, 512, 2, True),
            (1, 0, 512, 0, True), (1, 0, 512, 1, True), (1, 0, 512, 2, False),
            (1, 512, 512, 0, True), (1, 512, 512, 1, True), (1, 512, 256, 2, False), (1, 768, 256, 2, False),
        ]
        closes = [2,5,7,10]
        slots = [5,8,0,4,3,0,5,3,4,2,7,8,8.5]
        scaled = {}
        turned = {}
        active = {}
        totals = {}

        def gather(u):
            b, start, width, d, on_tensor = units[u]
            scaled[u] = placed.tile([P, units[u][2]], F32, name="scaled%d" % u, align_bytes=64, offset=int(2048 * slots[u]))
            offsets = lists[d][:, start // 16 : (start + width) // 16]
            nc.vector.tensor_tensor(
                scaled[u][:, :width], rows["h", b][:].indirect(offsets), rows["g", b][:, start : start + width], MULT
            )

        def turn_shift(u):
            b, start, width, d, on_tensor = units[u]
            turned[u] = psum.tile([P, HALF], F32, name="turned%d" % u, offset=2048 * BANKS["u" + str(u)])
            for j in range(width // P):
                nc.tensor.matmul(
                    turned[u][:, P * j : P * (j + 1)],
                    rows["s", b][:, start + P * j : start + P * (j + 1)],
                    identity[:],
                    start=(j == 0),
                    stop=False,
                    is_transpose=True,
                )

        def turn_scaled(u):
            b, start, width, d, on_tensor = units[u]
            for j in range(width // P):
                nc.tensor.matmul(
                    turned[u][:, P * j : P * (j + 1)],
                    scaled[u][:, P * j : P * (j + 1)],
                    identity[:],
                    start=False,
                    stop=(j == width // P - 1),
                    is_transpose=True,
                )
            active[u] = placed.tile([P, width], F32, name="active%d" % u, align_bytes=64, offset=2048 * (11 + u))
            nc.scalar.activation(active[u][:, :width], turned[u][:, :width], SILU)

        def turn_back(u):
            b, start, width, d, on_tensor = units[u]
            if d == 0:
                totals[b, start] = psum.tile([P, HALF], F32, name="total%d" % u, offset=2048 * BANKS["o" + str(u // 3)])
            total = totals[b, start]
            for j in range(width // P):
                nc.tensor.matmul(
                    total[:, P * j : P * (j + 1)],
                    active[u][:, P * j : P * (j + 1)],
                    identity[:],
                    start=(d == 0 and j == 0),
                    stop=(u in closes and j == width // P - 1),
                    is_transpose=True,
                )

        def store(u):
            b, start, width, d, on_tensor = units[u]
            result = keep.tile([P, width], F32, name="result%d" % u)
            nc.scalar.copy(out=result[:, :width], in_=totals[b, start][:, :width])
            nc.sync.dma_start(out=out[P * b : P * (b + 1), start : start + width], in_=result[:, :width])

        def shift_on_vector(u):
            b, start, width, d, on_tensor = units[u]
            shifted = placed.tile([P, width], F32, name="shifted%d" % u, align_bytes=64, offset=2048 * BANKS["y%d" % min(u, 11)] + 1024 * (u == 12))
            nc.vector.tensor_tensor(shifted[:, :width], scaled[u][:, :width], rows["s", b][:, start : start + width], ADD)
            active[u] = placed.tile([P, width], F32, name="active%d" % u, align_bytes=64, offset=2048 * BANKS["a%d" % min(u, 11)] + 1024 * (u == 12))
            nc.scalar.activation(active[u][:, :width], shifted[:, :width], SILU)

        def finish_on_vector(u):
            b, start, width, d, on_tensor = units[u]
            first = start - start % HALF
            result = keep.tile([P, width], F32, name="result%d" % u)
            nc.vector.tensor_tensor(
                result[:, :width], totals[b, first][:, start - first : start - first + width], active[u][:, :width], ADD
            )
            nc.sync.dma_start(out=out[P * b : P * (b + 1), start : start + width], in_=result[:, :width])

        load_w("g", 0, 0)
        load_x(0, 0)
        load_w("h", 0, 0)
        load_w("h", 0, 1)
        load_w("g", 0, 1)
        load_x(1, 0)
        load_w("s", 0, 0)
        load_x(0, 1)
        load_w("s", 0, 1)
        load_x(1, 1)
        load_w("h", 1, 1)
        load_list(0, pos1)
        load_w("g", 1, 0)
        load_w("s", 1, 0)
        load_list(1, pos2)
        load_w("h", 1, 0)
        load_list(2, pos3)
        load_w("g", 1, 1)
        load_w("s", 1, 1)
        cast("g", 0, 0, False)
        quantize("g", 0, 0)
        mx_pass("g", 0, 0, 0)
        cast("h", 0, 0, True)
        quantize("h", 0, 0)
        cast("h", 0, 1, True)
        mx_pass("h", 0, 0, 0)
        quantize("h", 0, 1)
        cast("g", 0, 1, True)
        mx_pass("h", 0, 0, 1)
        quantize("g", 0, 1)
        cast("s", 0, 0, False)
        mx_pass("g", 0, 0, 1)
        evacuate("h", 0, 0, True)
        mx_pass("h", 0, 1, 0)
        evacuate("g", 0, 0)
        quantize("s", 0, 0)
        cast("s", 0, 1, True)
        mx_pass("s", 0, 0, 0)
        quantize("s", 0, 1)
        mx_pass("h", 0, 1, 1)
        mx_pass("g", 0, 1, 0)
        mx_pass("g", 0, 1, 1)
        cast_wide("h", 1, False)
        evacuate("h", 0, 1, True)
        mx_pass("s", 0, 0, 1)
        evacuate("g", 0, 1)
        cast_wide("g", 0, True)
        mx_pass("s", 0, 1, 0)
        mx_pass("s", 0, 1, 1)
        gather(0)
        evacuate("s", 0, 0)
        cast_wide("s", 0, False)
        turn_shift(0)
        gather(1)
        cast_wide("h", 0, False)
        turn_shift(2)
        turn_scaled(0)
        evacuate("s", 0, 1)
        turn_shift(1)
        quantize_wide("h")
        cast_wide("g", 1, False)
        turn_scaled(1)
        gather(2)
        mx_pass("h", 1, 0, 0)
        mx_pass("h", 1, 0, 1)
        turn_back(0)
        cast_wide("s", 1, True)
        evacuate("h", 1, 0)
        quantize_wide("g")
        turn_scaled(2)
        gather(3)
        mx_pass("h", 1, 1, 0)
        mx_pass("h", 1, 1, 1)
        quantize_wide("s")
        turn_back(1)
        evacuate("h", 1, 1)
        turn_shift(3)
        gather(4)
        mx_pass("g", 1, 0, 0)
        mx_pass("g", 1, 0, 1)
        turn_scaled(3)
        gather(5)
        evacuate("g", 1, 0)
        turn_shift(4)
        turn_back(2)
        turn_shift(5)
        gather(6)
        store(2)
        turn_scaled(4)
        mx_pass("s", 1, 0, 0)
        mx_pass("s", 1, 0, 1)
        gather(8)
        turn_scaled(5)
        evacuate("s", 1, 0)
        turn_back(3)
        turn_back(4)
        mx_pass("g", 1, 1, 0)
        mx_pass("g", 1, 1, 1)
        gather(7)
        turn_back(5)
        evacuate("g", 1, 1)
        turn_shift(6)
        shift_on_vector(8)
        turn_scaled(6)
        store(5)
        mx_pass("s", 1, 1, 0)
        mx_pass("s", 1, 1, 1)
        gather(9)
        turn_shift(7)
        evacuate("s", 1, 1)
        turn_back(6)
        gather(10)
        turn_scaled(7)
        turn_shift(10)
        turn_shift(9)
        turn_scaled(9)
        gather(12)
        turn_scaled(10)
        turn_back(7)
        gather(11)
        shift_on_vector(12)
        turn_back(9)
        shift_on_vector(11)
        finish_on_vector(8)
        turn_back(10)
        finish_on_vector(12)
        finish_on_vector(11)
